import numpy as np
import ml_dtypes

BF16 = ml_dtypes.bfloat16


def bf(x):
    return np.asarray(x, np.float32).astype(BF16)


def f32(x):
    return np.asarray(x, np.float32)


def f64(x):
    return np.asarray(x).astype(np.float64)


def striped(idx):
    return np.tile(idx.reshape(-1, 16).T, (8, 1))


S, K, M, N, E, Q = 256, 128, 256, 512, 4, 128


def sigmoid(v):
    return 1.0 / (1.0 + np.exp(-v))


def two_experts():
    first = np.random.permutation(S).reshape(E, S // E)
    return np.concatenate([np.random.permutation(np.concatenate([first[e], first[(e + 1) % E]])) for e in range(E)])


def setup_inputs():
    return {"table": bf(np.random.standard_normal((K, S))), "w": bf(np.random.standard_normal((E, K, M)) / np.sqrt(K)), "b": f32(0.5 * np.random.standard_normal((M, 1))), "offs": striped(two_experts())}


def reference(table, w, b, offs):
    idx = offs[:16].T.reshape(-1)
    x = f64(table)[:, idx]
    y = np.concatenate([f64(w)[e].T @ x[:, e * Q : (e + 1) * Q] for e in range(E)], axis=1)
    return (y + f64(b)) * sigmoid(y + f64(b))

@@ -1,0 +1,47 @@
+import concourse.mybir as mybir
+
+BF16, F32, U16 = mybir.dt.bfloat16, mybir.dt.float32, mybir.dt.uint16
+SILU = mybir.ActivationFunctionType.Silu
+
+P = 128
+S = 256
+M = 256
+E = 4
+Q = 128
+N = E * Q
+M_BLOCKS = M // P
+Q_COLS = Q // 16
+
+FLOPS = 2 * P * M * N
+
+
+def tile_gather_matmul_kernel(tc, table, w, b, offs, out):
+    nc = tc.nc
+    with (
+        tc.tile_pool(name="held", bufs=1) as held,
+        tc.psum_pool(name="psum", bufs=1) as psum,
+    ):
+        offsets = held.tile([P, N // 16], U16, name="offsets")
+        nc.sync.dma_start(offsets[:], offs)
+        tokens = held.tile([P, S], BF16, name="tokens")
+        nc.sync.dma_start(tokens[:], table)
+        weights = held.tile([P, E, M], BF16, name="weights")
+        nc.scalar.dma_start(weights[:], w.rearrange("e k m -> k e m"))
+        bias = held.tile([P, M_BLOCKS], F32, name="bias")
+        with nc.allow_non_contiguous_dma(reason="one float32 bias value to a partition"):
+            nc.gpsimd.dma_start(bias[:], b.rearrange("(a p) o -> p (a o)", p=P))
+
+        for a in range(M_BLOCKS):
+            bank = psum.tile([P, N], F32, name=f"bank{a}")
+            for e in range(E):
+                picked = tokens[:].indirect(offsets[:, e * Q_COLS : (e + 1) * Q_COLS])
+                nc.tensor.matmul(
+                    bank[:, e * Q : (e + 1) * Q],
+                    weights[:, e, a * P : (a + 1) * P],
+                    picked,
+                    start=True,
+                    stop=True,
+                )
+            acted = held.tile([P, N], F32, name=f"acted{a}")
+            nc.scalar.activation(acted[:], bank[:], SILU, bias=bias[:, a : a + 1])
+            nc.sync.dma_start(out[a * P : (a + 1) * P, :], acted[:])

@@ -19,29 +19,31 @@ def tile_gather_matmul_kernel(tc, table, w, b, offs, out):
     nc = tc.nc
     with (
         tc.tile_pool(name="held", bufs=1) as held,
-        tc.psum_pool(name="psum", bufs=1) as psum,
+        tc.tile_pool(name="results", bufs=E * M_BLOCKS) as results,
+        tc.psum_pool(name="psum", bufs=E * M_BLOCKS) as psum,
     ):
         offsets = held.tile([P, N // 16], U16, name="offsets")
         nc.sync.dma_start(offsets[:], offs)
+        weights = [held.tile([P, M], BF16, name=f"weights{e}") for e in range(E)]
+        nc.scalar.dma_start(weights[0][:], w[0])
         tokens = held.tile([P, S], BF16, name="tokens")
         nc.sync.dma_start(tokens[:], table)
-        weights = held.tile([P, E, M], BF16, name="weights")
-        nc.scalar.dma_start(weights[:], w.rearrange("e k m -> k e m"))
         bias = held.tile([P, M_BLOCKS], F32, name="bias")
         with nc.allow_non_contiguous_dma(reason="one float32 bias value to a partition"):
-            nc.gpsimd.dma_start(bias[:], b.rearrange("(a p) o -> p (a o)", p=P))
+            nc.scalar.dma_start(bias[:], b.rearrange("(a p) o -> p (a o)", p=P))
+        nc.sync.dma_start(weights[1][:], w[1])
+        nc.scalar.dma_start(weights[2][:], w[2])
+        nc.sync.dma_start(weights[3][:], w[3])
 
-        for a in range(M_BLOCKS):
-            bank = psum.tile([P, N], F32, name=f"bank{a}")
-            for e in range(E):
-                picked = tokens[:].indirect(offsets[:, e * Q_COLS : (e + 1) * Q_COLS])
-                nc.tensor.matmul(
-                    bank[:, e * Q : (e + 1) * Q],
-                    weights[:, e, a * P : (a + 1) * P],
-                    picked,
-                    start=True,
-                    stop=True,
-                )
-            acted = held.tile([P, N], F32, name=f"acted{a}")
-            nc.scalar.activation(acted[:], bank[:], SILU, bias=bias[:, a : a + 1])
-            nc.sync.dma_start(out[a * P : (a + 1) * P, :], acted[:])
+        scratch = held.tile([P, 1], F32, name="scratch")
+        nc.vector.memset(scratch[:], 0.0)
+        nc.scalar.activation(scratch[:], scratch[:], SILU)
+
+        for e in range(E):
+            picked = tokens[:].indirect(offsets[:, e * Q_COLS : (e + 1) * Q_COLS])
+            for a in range(M_BLOCKS):
+                bank = psum.tile([P, Q], F32)
+                nc.tensor.matmul(bank[:], weights[e][:, a * P : (a + 1) * P], picked, start=True, stop=True)
+                acted = results.tile([P, Q], F32)
+                nc.scalar.activation(acted[:], bank[:], SILU, bias=bias[:, a : a + 1])
+                nc.sync.dma_start(out[a * P : (a + 1) * P, e * Q : (e + 1) * Q], acted[:])

@@ -22,12 +22,12 @@ def tile_gather_matmul_kernel(tc, table, w, b, offs, out):
         tc.tile_pool(name="results", bufs=E * M_BLOCKS) as results,
         tc.psum_pool(name="psum", bufs=E * M_BLOCKS) as psum,
     ):
-        offsets = held.tile([P, N // 16], U16, name="offsets")
-        nc.sync.dma_start(offsets[:], offs)
-        weights = [held.tile([P, M], BF16, name=f"weights{e}") for e in range(E)]
-        nc.scalar.dma_start(weights[0][:], w[0])
         tokens = held.tile([P, S], BF16, name="tokens")
         nc.sync.dma_start(tokens[:], table)
+        weights = [held.tile([P, M], BF16, name=f"weights{e}") for e in range(E)]
+        nc.scalar.dma_start(weights[0][:], w[0])
+        offsets = held.tile([P, N // 16], U16, name="offsets")
+        nc.sync.dma_start(offsets[:], offs)
         bias = held.tile([P, M_BLOCKS], F32, name="bias")
         with nc.allow_non_contiguous_dma(reason="one float32 bias value to a partition"):
             nc.scalar.dma_start(bias[:], b.rearrange("(a p) o -> p (a o)", p=P))

@@ -29,8 +29,7 @@ def tile_gather_matmul_kernel(tc, table, w, b, offs, out):
         offsets = held.tile([P, N // 16], U16, name="offsets")
         nc.sync.dma_start(offsets[:], offs)
         bias = held.tile([P, M_BLOCKS], F32, name="bias")
-        with nc.allow_non_contiguous_dma(reason="one float32 bias value to a partition"):
-            nc.scalar.dma_start(bias[:], b.rearrange("(a p) o -> p (a o)", p=P))
+        nc.scalar.dma_start(bias[:], b.rearrange("(p a) o -> p (a o)", a=M_BLOCKS))
         nc.sync.dma_start(weights[1][:], w[1])
         nc.scalar.dma_start(weights[2][:], w[2])
         nc.sync.dma_start(weights[3][:], w[3])
@@ -39,11 +38,12 @@ def tile_gather_matmul_kernel(tc, table, w, b, offs, out):
         nc.vector.memset(scratch[:], 0.0)
         nc.scalar.activation(scratch[:], scratch[:], SILU)
 
+        out_blocks = out.rearrange("(p a) n -> p a n", a=M_BLOCKS)
         for e in range(E):
             picked = tokens[:].indirect(offsets[:, e * Q_COLS : (e + 1) * Q_COLS])
             for a in range(M_BLOCKS):
                 bank = psum.tile([P, Q], F32)
-                nc.tensor.matmul(bank[:], weights[e][:, a * P : (a + 1) * P], picked, start=True, stop=True)
+                nc.tensor.matmul(bank[:], weights[e][:, a:M:M_BLOCKS], picked, start=True, stop=True)
                 acted = results.tile([P, Q], F32)
                 nc.scalar.activation(acted[:], bank[:], SILU, bias=bias[:, a : a + 1])
-                nc.sync.dma_start(out[a * P : (a + 1) * P, e * Q : (e + 1) * Q], acted[:])
+                nc.sync.dma_start(out_blocks[:, a, e * Q : (e + 1) * Q], acted[:])

import concourse.mybir as mybir

BF16, F32, U16 = mybir.dt.bfloat16, mybir.dt.float32, mybir.dt.uint16
SILU = mybir.ActivationFunctionType.Silu

P = 128
S = 256
M = 256
E = 4
Q = 128
N = E * Q
M_BLOCKS = M // P
Q_COLS = Q // 16

FLOPS = 2 * P * M * N


def tile_gather_matmul_kernel(tc, table, w, b, offs, out):
    nc = tc.nc
    with (
        tc.tile_pool(name="held", bufs=1) as held,
        tc.tile_pool(name="results", bufs=E * M_BLOCKS) as results,
        tc.psum_pool(name="psum", bufs=E * M_BLOCKS) as psum,
    ):
        tokens = held.tile([P, S], BF16, name="tokens")
        nc.sync.dma_start(tokens[:], table)
        weights = [held.tile([P, M], BF16, name=f"weights{e}") for e in range(E)]
        nc.scalar.dma_start(weights[0][:], w[0])
        offsets = held.tile([P, N // 16], U16, name="offsets")
        nc.sync.dma_start(offsets[:], offs)
        bias = held.tile([P, M_BLOCKS], F32, name="bias")
        nc.scalar.dma_start(bias[:], b.rearrange("(p a) o -> p (a o)", a=M_BLOCKS))
        nc.sync.dma_start(weights[1][:], w[1])
        nc.scalar.dma_start(weights[2][:], w[2])
        nc.sync.dma_start(weights[3][:], w[3])

        scratch = held.tile([P, 1], F32, name="scratch")
        nc.vector.memset(scratch[:], 0.0)
        nc.scalar.activation(scratch[:], scratch[:], SILU)

        out_blocks = out.rearrange("(p a) n -> p a n", a=M_BLOCKS)
        for e in range(E):
            picked = tokens[:].indirect(offsets[:, e * Q_COLS : (e + 1) * Q_COLS])
            for a in range(M_BLOCKS):
                bank = psum.tile([P, Q], F32)
                nc.tensor.matmul(bank[:], weights[e][:, a:M:M_BLOCKS], picked, start=True, stop=True)
                acted = results.tile([P, Q], F32)
                nc.scalar.activation(acted[:], bank[:], SILU, bias=bias[:, a : a + 1])
                nc.sync.dma_start(out_blocks[:, a, e * Q : (e + 1) * Q], acted[:])
